import numpy as np
import ml_dtypes


def mxq(x, axis, fmt="e4m3"):
    dtype, down = {"e4m3": (ml_dtypes.float8_e4m3fn, 7), "e5m2": (ml_dtypes.float8_e5m2, 14)}[fmt]
    v = np.moveaxis(np.asarray(x, np.float32).astype(ml_dtypes.bfloat16).astype(np.float64), axis, -1)
    blocks = v.reshape(v.shape[:-1] + (-1, 32))
    amax = np.abs(blocks).max(-1, keepdims=True)
    byte = np.maximum(np.where(amax > 0, np.frexp(amax)[1] - 1 + 127, 0) - down, 1)
    scale = np.exp2(byte - 127.0)
    codes = (blocks / scale).astype(np.float32).astype(dtype).astype(np.float64)
    return np.moveaxis((codes * scale).reshape(v.shape), -1, axis)


WIDE = False


def mx_kscale(k):
    if not WIDE:
        return np.ones(k)
    levels = np.array([10, -10, 5, -5, 0])
    if k % 512:
        return np.exp2(np.random.permutation(np.resize(levels, k // 32))).repeat(32)
    a = np.empty((k // 512, 16))
    for p in range(k // 512):
        a[p, :8] = np.random.permutation(np.resize(levels, 8))
        for g in range(8):
            far = levels[np.abs(levels - a[p, g]) >= 10]
            a[p, g + 8] = far[np.random.randint(len(far))]
    return np.exp2(a.ravel()).repeat(32)


def f64(x):
    return np.asarray(x).astype(np.float64)


def striped(idx):
    return np.tile(np.asarray(idx).reshape(-1, 16).T, (8, 1)).astype(np.uint16)


def unstriped(offs):
    return offs[:16].T.reshape(-1).astype(np.int64)


E2M1 = np.array([0.0, 0.5, 1.0, 1.5, 2.0, 3.0, 4.0, 6.0, -0.0, -0.5, -1.0, -1.5, -2.0, -3.0, -4.0, -6.0])


def pack_weight(w, fmt):
    k, n = w.shape
    w = f64(np.asarray(w, np.float32).astype(ml_dtypes.bfloat16)).reshape(k // 32, 32, n)
    amax = np.abs(w).max(1)
    if fmt == "e4m3":
        byte = np.frexp(amax)[1] - 1 + 127 - 7
    else:
        mant, ex = np.frexp(amax / 6.0)
        byte = np.where(mant > 0.5, ex, ex - 1) + 127
    byte = np.clip(np.where(amax > 0, byte, 1), 1, 254)
    scaled = (w * np.exp2(127.0 - byte)[:, None, :]).reshape(k, n).astype(np.float32)
    by_word = np.ascontiguousarray(scaled.reshape(k // 512, 128, 4, n).transpose(0, 1, 3, 2))
    if fmt == "e4m3":
        words = by_word.astype(ml_dtypes.float8_e4m3fn).view(np.uint8)
    else:
        c = by_word.astype(ml_dtypes.float4_e2m1fn).view(np.uint8) & 0xF
        words = (c[..., 0::2] | (c[..., 1::2] << 4)).reshape(k // 512, 128, 2 * n)
    return np.ascontiguousarray(words), np.ascontiguousarray(byte.astype(np.uint8).reshape(k // 512, 16, n))


def unpack_weight(words, scales, fmt):
    g, _, n = scales.shape
    words = np.ascontiguousarray(words).reshape(g, 128, n, -1)
    if fmt == "e4m3":
        vals = words.view(ml_dtypes.float8_e4m3fn).astype(np.float64)
    else:
        nib = np.empty((g, 128, n, 4), np.uint8)
        nib[..., 0::2] = words & 0xF
        nib[..., 1::2] = words >> 4
        vals = E2M1[nib]
    vals = vals * np.repeat(np.exp2(scales.astype(np.float64) - 127.0), 8, axis=1)[..., None]
    return vals.transpose(0, 1, 3, 2).reshape(g * 512, n)


D, T, I, Q, H, U, G, M = 512, 2048, 512, 128, 512, 1024, 64, 512


def setup_inputs():
    n = np.random.standard_normal
    idx = np.random.permutation(T)[:I]
    idx2 = np.random.permutation(U)[:I]
    idx3 = np.random.permutation(M)[:G]
    fh = mx_kscale(H)
    fd = mx_kscale(D)
    keysp = pack_weight(n((D, T)) / fd[:, None], "e2m1")
    return {
        "query": (n((H, Q)) * 1.0 / np.sqrt(H) / fh[:, None]).astype(np.float32),
        "wk": (n((D, H)) * 0.7 / np.sqrt(D) * fd[:, None] * fh).astype(np.float32),
        "wk2": (n((D, H)) * 0.7 / np.sqrt(D) * fd[:, None] * fh).astype(np.float32),
        "keys_words": keysp[0],
        "keys_scales": keysp[1],
        "parts": (n((D, U)) / fd[:, None]).astype(np.float32),
        "worth": np.tile(np.random.uniform(0.2, 2.0, T), (128, 1)).astype(np.float32),
        "old": (1.0 * n((Q, M))).astype(np.float32),
        "offs": striped(idx),
        "offs2": striped(idx2),
        "offs3": striped(idx3),
    }


def reference(query, wk, wk2, keys_words, keys_scales, parts, worth, old, offs, offs2, offs3):
    idx = unstriped(offs)
    idx2 = unstriped(offs2)
    idx3 = unstriped(offs3)
    keysu = unpack_weight(keys_words, keys_scales, "e2m1")
    wkq = mxq(f64(wk), 0, "e4m3")
    keysidxg = keysu[:, idx]
    wk2q = mxq(f64(wk2), 0, "e4m3")
    partsidx2q = mxq(f64(parts)[:, idx2], 0, "e4m3")
    kp = wkq.T @ keysidxg + wk2q.T @ partsidx2q
    queryq = mxq(f64(query), 0, "e4m3")
    kpq = mxq(kp, 0, "e4m3")
    s = queryq.T @ kpq
    w = np.maximum(s, 0.0)
    ws = w * f64(worth)[:1][:, idx] * 2.0
    wp = ws.reshape(Q, G, I // G).sum(axis=2)
    wf = np.zeros((Q, M))
    wf[:, idx3] = wp
    y = f64(old) + wf
    return y

from contextlib import ExitStack

import concourse.mybir as mybir
from concourse.masks import make_identity

D, T, I, Q, H, U, G, M = 512, 2048, 512, 128, 512, 1024, 64, 512
P = 128
PACK = 4
RUN = I // G
QUARTERS = I // P

F32 = mybir.dt.float32
BF16 = mybir.dt.bfloat16
I32 = mybir.dt.int32
U32 = mybir.dt.uint32
U16 = mybir.dt.uint16
U8 = mybir.dt.uint8
FP8X4 = mybir.dt.float8_e4m3fn_x4
FP4X4 = mybir.dt.float4_e2m1fn_x4
COPY = mybir.ActivationFunctionType.Copy
ALU = mybir.AluOpType
AXIS_X = mybir.AxisListType.X

FLOPS = 2 * (2 * D * H * I + H * Q * I)
BYTES = 4 * (H * Q + 2 * D * H + D * U + T + 2 * Q * M) + P * 2 * T + 16 * T + 2 * P * (2 * I + G) // 16

WK2_VECTOR_COLUMNS = 88
WK_VECTOR_COLUMNS = 72


def quantize(nc, pool, name, grouped, width):
    codes = pool.tile([P, width], U32, name=name + "_codes", align_bytes=64)
    scales = pool.tile([P, width], U8, name=name + "_scales", align_bytes=64)
    nc.vector.quantize_mx(out=codes[:].bitcast(FP8X4), scales=scales[:], in_=grouped)
    return codes, scales


def deal_matrix(nc, pool, name, raw, vector_columns):
    grouped = pool.tile([P, PACK, P, PACK], BF16, name=name + "_grouped", tag=name + "_grouped", align_bytes=64)
    source = raw[:].rearrange("p j (m t) -> p m j t", t=PACK)
    target = grouped[:].rearrange("p t m j -> p m j t")
    nc.scalar.copy(target[:, vector_columns:], source[:, vector_columns:])
    nc.vector.tensor_copy(target[:, :vector_columns], source[:, :vector_columns])
    return grouped[:].rearrange("p t m j -> p (t m j)")


def tile_attend_composedkeys_pagesums_lean_kernel(
    tc, query, wk, wk2, keys_words, keys_scales, parts, worth, old, offs, offs2, offs3, out
):
    nc = tc.nc
    with ExitStack() as ctx:
        lists = ctx.enter_context(tc.tile_pool(name="lists", bufs=1))
        pool = ctx.enter_context(tc.tile_pool(name="pool", bufs=1))
        psum = ctx.enter_context(tc.psum_pool(name="psum", bufs=1))

        token_list = lists.tile([P, I // 16], U16)
        part_list = lists.tile([P, I // 16], U16)
        column_list = lists.tile([P, G // 16], U16)

        key_scale_pool = pool.tile([P, T], U8, align_bytes=64)
        worth_pool = pool.tile([P, T], F32, tag="wk_grouped", align_bytes=64)
        placed = pool.tile([P, M], F32)
        identity = pool.tile([P, P], F32)
        nc.vector.memset(worth_pool[:, : T // 2], 0.0)
        nc.gpsimd.memset(worth_pool[:, T // 2 :], 0.0)
        nc.vector.memset(key_scale_pool[:].bitcast(I32), 0)
        make_identity(nc, identity[:])
        nc.gpsimd.memset(placed[:], 0.0)

        part_rows = parts.rearrange("(p j) u -> p j u", j=PACK)
        part_pool = [pool.tile([P, U], F32, name="part_pool%d" % j, tag="part_pool%d" % j) for j in range(PACK)]
        wk2_raw = pool.tile([P, PACK, H], F32)
        wk_raw = pool.tile([P, PACK, H], F32, tag="wk_bytes", align_bytes=64)
        query_raw = pool.tile([P, PACK, Q], F32)
        key_word_pool = pool.tile([P, T], U16, align_bytes=64)
        old_sums = pool.tile([P, M], F32)
        nc.sync.dma_start(token_list[:], offs)
        nc.sync.dma_start(wk2_raw[:], wk2.rearrange("(p j) h -> p j h", j=PACK))
        nc.sync.dma_start(part_list[:], offs2)
        nc.sync.dma_start(part_pool[0][:], part_rows[:, 0, :])
        nc.sync.dma_start(worth_pool[0:1, :], worth[0:1, :])
        nc.sync.dma_start(part_pool[1][:], part_rows[:, 1, :])
        scale_words = keys_scales[0].bitcast(I32)
        for quadrant in range(4):
            nc.sync.dma_start(
                key_scale_pool[32 * quadrant : 32 * quadrant + 4, :].bitcast(I32),
                scale_words[4 * quadrant : 4 * quadrant + 4, :],
            )
        for j in range(2, PACK):
            nc.sync.dma_start(part_pool[j][:], part_rows[:, j, :])
        nc.sync.dma_start(wk_raw[:], wk.rearrange("(p j) h -> p j h", j=PACK))
        nc.sync.dma_start(query_raw[:], query.rearrange("(p j) q -> p j q", j=PACK))
        nc.sync.dma_start(key_word_pool[:].bitcast(I32), keys_words[0].bitcast(I32))
        nc.sync.dma_start(old_sums[:], old)
        nc.sync.dma_start(column_list[:], offs3)

        wk2_codes, wk2_scales = quantize(nc, pool, "wk2", deal_matrix(nc, pool, "wk2", wk2_raw, WK2_VECTOR_COLUMNS), H)

        half = I // 2
        part_planes = [pool.tile([P, PACK, half], F32, name="part_planes%d" % a, tag=("planes", "wk_grouped")[a], align_bytes=64) for a in range(2)]
        key_scales = pool.tile([P, I], U8, align_bytes=64)
        worth_row = pool.tile([P, I], F32)

        def gather_plane(j, a, on_vector):
            picked = part_pool[j][:].indirect(part_list[:, a * half // 16 : (a + 1) * half // 16])
            if on_vector:
                nc.vector.tensor_copy(part_planes[a][:, j, :], picked)
            else:
                nc.scalar.activation(part_planes[a][:, j, :], picked, COPY)

        nc.scalar.activation(worth_row[:], worth_pool[:].indirect(token_list[:]), COPY)
        for j in range(PACK):
            gather_plane(j, 0, True)
            gather_plane(j, 1, False)
            if j == 1:
                nc.vector.tensor_copy(key_scales[:], key_scale_pool[:].indirect(token_list[:]))

        worth_turned = psum.tile([P, QUARTERS, P], F32, tag="bank1")
        for c in range(QUARTERS):
            nc.tensor.transpose(worth_turned[:, c, :], worth_row[:, c * P : (c + 1) * P], identity[:])
        worth_columns = pool.tile([P, QUARTERS], F32, tag="part_pool1")
        nc.scalar.activation(worth_columns[:], worth_turned[:, :, 0], COPY, scale=2.0)
        worth_spread = psum.tile([P, QUARTERS, P], F32, tag="bank0")
        for c in range(QUARTERS):
            nc.tensor.transpose(worth_spread[:, c, :], worth_columns[:, c : c + 1].to_broadcast([P, P]), identity[:])
        twice_worth = pool.tile([P, QUARTERS, P], F32, tag="part_pool2")
        nc.scalar.copy(twice_worth[:], worth_spread[:])

        banks = [psum.tile([P, PACK, P], F32, name="bank%d" % c, tag="bank%d" % c) for c in range(QUARTERS)]

        part_mx = []
        for a in range(2):
            part_grouped = pool.tile([P, half, PACK], BF16, name="part_grouped%d" % a, align_bytes=64)
            nc.vector.tensor_copy(
                part_grouped[:].rearrange("p (c i) j -> p c j i", i=4),
                part_planes[a][:].rearrange("p j (c i) -> p c j i", i=4),
            )
            part_mx.append(quantize(nc, pool, "part%d" % a, part_grouped[:].rearrange("p i j -> p (i j)"), half))
        for c in range(QUARTERS):
            part_codes, part_scales = part_mx[c // 2]
            slots = slice(c % 2 * P, (c % 2 + 1) * P)
            for t in range(PACK):
                cols = slice(t * P, (t + 1) * P)
                nc.tensor.matmul_mx(
                    out=banks[c][:, t, :],
                    lhsT=wk2_codes[:, cols].bitcast(FP8X4),
                    lhsT_scale=wk2_scales[:, cols],
                    rhs=part_codes[:, slots].bitcast(FP8X4),
                    rhs_scale=part_scales[:, slots],
                    start=(t == 0),
                    stop=False,
                )

        wk_codes, wk_scales = quantize(nc, pool, "wk", deal_matrix(nc, pool, "wk", wk_raw, WK_VECTOR_COLUMNS), H)

        query_grouped = pool.tile([P, Q, PACK], BF16, tag="wk_bytes", align_bytes=64)
        nc.scalar.copy(
            query_grouped[:].rearrange("p (c i) j -> p c j i", i=4),
            query_raw[:].rearrange("p j (c i) -> p c j i", i=4),
        )

        key_words = pool.tile([P, I], U16, tag="wk_grouped", align_bytes=64)
        for a in range(2):
            nc.vector.tensor_copy(
                key_words[:, a * half : (a + 1) * half], key_word_pool[:].indirect(token_list[:, a * half // 16 : (a + 1) * half // 16])
            )
        for c in range(QUARTERS):
            slots = slice(c * P, (c + 1) * P)
            for t in range(PACK):
                cols = slice(t * P, (t + 1) * P)
                nc.tensor.matmul_mx(
                    out=banks[c][:, t, :],
                    lhsT=wk_codes[:, cols].bitcast(FP8X4),
                    lhsT_scale=wk_scales[:, cols],
                    rhs=key_words[:, slots].bitcast(FP4X4),
                    rhs_scale=key_scales[:, slots],
                    start=False,
                    stop=(t == PACK - 1),
                )
        query_codes, query_scales = quantize(nc, pool, "query", query_grouped[:].rearrange("p q j -> p (q j)"), Q)

        run_sums = pool.tile([P, G], F32)
        runs = P // RUN
        grouped = []
        for c in range(QUARTERS):
            key_grouped = pool.tile([P, P, PACK], BF16, name="key_grouped%d" % c, align_bytes=64)
            turned = banks[c][:].rearrange("p t i -> p i t")
            if c == 1:
                nc.vector.tensor_copy(key_grouped[:], turned)
            else:
                nc.scalar.copy(key_grouped[:], turned)
            grouped.append(key_grouped)
        for c in range(QUARTERS):
            codes, scales = quantize(nc, pool, "key%d" % c, grouped[c][:].rearrange("p i t -> p (i t)"), P)
            nc.tensor.matmul_mx(
                out=banks[c][:, 0, :],
                lhsT=query_codes[:].bitcast(FP8X4),
                lhsT_scale=query_scales[:],
                rhs=codes[:].bitcast(FP8X4),
                rhs_scale=scales[:],
                start=True,
                stop=True,
            )
        for c in range(QUARTERS):
            weighted = pool.tile([P, runs, RUN], F32, name="weighted%d" % c)
            nc.vector.scalar_tensor_tensor(
                weighted[:].rearrange("p g r -> p (g r)"), banks[c][:, 0, :], 0.0, twice_worth[:, c, :], ALU.max, ALU.mult
            )
            nc.vector.tensor_reduce(run_sums[:, c * runs : (c + 1) * runs], weighted[:], AXIS_X, ALU.add)

        nc.vector.tensor_copy(placed[:].indirect(column_list[:]), run_sums[:])
        for a, queue in enumerate((nc.sync, nc.scalar)):
            cols = slice(a * M // 2, (a + 1) * M // 2)
            result = pool.tile([P, M // 2], F32, name="result%d" % a)
            nc.vector.tensor_tensor(result[:], placed[:, cols], old_sums[:, cols], ALU.add)
            queue.dma_start(out[:, cols], result[:])
